import numpy as np, ml_dtypes
CORES = [4,20,60,84,92,100,116]
N = 7
import mx_ref
NC = 320
CNT = [[32,0,0,0,160,0,128],[48,0,0,144,48,80,0],[32,0,96,128,64,0,0],[144,0,0,16,80,80,0],[64,112,80,0,64,0,0],[48,80,96,0,96,0,0],[80,0,96,0,0,64,80]]
OFF = [[sum(c[:e]) for e in range(N + 1)] for c in CNT]
TOT = [sum(c[e] for c in CNT) for e in range(N)]
BF = ml_dtypes.bfloat16
def setup_inputs(rng):
    def f(*shape):
        return mx_ref.flush((rng.standard_normal(shape, dtype=np.float32) * np.exp2(rng.integers(-2, 3, shape[:-1] + (1,)))).astype(BF))
    return {"w": f(N, 128, 512), "x": f(N, 128, 4 * NC)}
def setup_inputs_blocks(rng):
    d = setup_inputs(rng)
    for k in ("w", "x"): d[k] = mx_ref.spread(d[k], rng, 4)
    return d
def setup_inputs_wide(rng):
    d = setup_inputs(rng)
    for k in ("w", "x"): d[k] = mx_ref.flush((d[k].astype(np.float32) * np.exp2(rng.integers(-10, 11, (N, 1, 1))).astype(np.float32)).astype(BF))
    return d
def setup_inputs_zeros(rng):
    d = setup_inputs(rng); v = d["x"].reshape(N, 128, -1, 4).copy()
    v[np.broadcast_to((rng.random((N, 1, v.shape[2], 1)) < 0.33), v.shape)] = 0
    d["x"] = v.reshape(d["x"].shape)
    return d
def reference(w, x):
    y = np.full((N, 128, max(TOT)), np.nan, np.float32)
    for e in range(N):
        t = np.concatenate([x[j][:, 4 * OFF[j][e]:4 * OFF[j][e + 1]] for j in range(N)], axis=1)
        y[e][:, :TOT[e]] = mx_ref.matmul(mx_ref.quantize(w[e]), mx_ref.quantize(t))
    return {"y": y}

from concourse.bass import DstId, RemoteDMATransfer
from concourse.mybir import dt, ActivationFunctionType

LEAST = 128
BANK = 512
E_HOP1 = 8
E_HOP2 = 8
E_DIRECT = 8
MAX_DIRECT = 2

SCRATCH = {
    "xb": ("sbuf", [128, 1280], "bfloat16"),
    "wb": ("sbuf", [128, 512], "bfloat16"),
    "xq": ("sbuf", [128, 320], "float8_e4m3fn_x4"),
    "xs": ("sbuf", [128, 320], "uint8"),
    "wq": ("sbuf", [128, 128], "float8_e4m3fn_x4"),
    "ws": ("sbuf", [128, 128], "uint8"),
    "hq": ("sbuf", [128, 320], "float8_e4m3fn_x4"),
    "hs": ("sbuf", [128, 320], "uint8"),
    "lq": ("sbuf", [128, 512], "float8_e4m3fn_x4"),
    "ls": ("sbuf", [128, 512], "uint8"),
    "ps": ("psum", [128, 2048], "float32"),
    "so": ("sbuf", [128, 128], "float32"),
    "sg": ("sbuf", [128, 512], "float32"),
}
SEMAPHORES = ["ld0", "ld1", "ldw", "q0", "q1", "qw", "sent", "hin0", "hin1",
              "arr0", "arr1", "arr2", "mmo", "mm0", "mm1", "mm2", "cpo", "cp0", "cp1", "cp2", "st"]


def _engines(mask, k, skip=0):
    out, b = 0, 0
    while k > 0:
        if (mask >> b) & 1:
            if skip > 0:
                skip -= 1
            else:
                out |= 1 << b
                k -= 1
        b += 1
    return out


def _plan(T, topo):
    cnt = T.tables["CNT"]
    cores = list(T.cores)
    n = len(cores)
    off = [[sum(r[:e]) for e in range(n + 1)] for r in cnt]
    tot = [sum(cnt[j][e] for j in range(n)) for e in range(n)]
    ncol = off[0][n]
    flows = [(j, e) for j in range(n) for e in range(n) if j != e and cnt[j][e] > 0]

    must = [f for f in flows if not topo.may_write(cores[f[0]], cores[f[1]])]
    relayed = list(must)
    waits_anyway = [any(f[1] == e for f in must) for e in range(n)]
    for j in range(n):
        direct = [e for (i, e) in flows if i == j and (i, e) not in relayed]
        mine = [e for (i, e) in relayed if i == j]
        while len(direct) > MAX_DIRECT and mine:
            cand = [e for e in direct if not waits_anyway[e]
                    and any(off[j][e] == off[j][r + 1] or off[j][e + 1] == off[j][r] for r in mine)]
            if not cand:
                break
            relayed.append((j, cand[0]))
            mine.append(cand[0])
            direct.remove(cand[0])

    helpers = {}
    for j in range(n):
        dests = [cores[e] for (i, e) in relayed if i == j]
        if not dests:
            continue
        c0 = cores[j]
        cand = [c for c in range(topo.CHIPS * topo.CORES_PER_CHIP)
                if topo.chip(c) == topo.chip(c0) and T.rank_of(c) is None and all(topo.may_write(c, d) for d in dests)]
        cand.sort(key=lambda c: (topo.die(c) != topo.die(c0), c))
        helpers[j] = (cand[0], cand[1])

    pieces, hulls, turn, eng = [], [], {}, {}
    for j in range(n):
        rel = [(off[j][e], off[j][e + 1], e) for (i, e) in relayed if i == j]
        best = None
        for e in range(1, n):
            c = off[j][e]
            if LEAST <= c <= ncol - LEAST:
                for first, second in (((0, c), (c, ncol)), ((c, ncol), (0, c))):
                    inside = sum(b - a for (a, b, _e) in rel if first[0] <= a and b <= first[1])
                    key = (-inside, first[1] - first[0])
                    if best is None or key < best[0]:
                        best = (key, [first, second])
        pj = best[1] if best else [(0, ncol)]
        pieces.append(pj)
        hj = []
        for p, (pa, pb) in enumerate(pj):
            runs = [r for r in rel if pa <= r[0] and r[1] <= pb]
            if runs:
                order = sorted(runs, key=lambda r: ((j, r[2]) not in must, r[0] - r[1]))
                calls = []
                for r in order:
                    if calls and len(calls[-1]) < 2 and cnt[j][calls[-1][0]] == r[1] - r[0]:
                        calls[-1].append(r[2])
                    else:
                        calls.append([r[2]])
                hj.append((p, min(r[0] for r in runs), max(r[1] for r in runs), calls))
        hulls.append(hj)
        t = 0
        for h in hj:
            for call in h[3]:
                for e in call:
                    turn[(j, e)] = t
                    eng[(j, e)] = E_HOP2 // len(call)
                t += 1

    experts = []
    for e in range(n):
        segs, y = [], 0
        for j in range(n):
            c = cnt[j][e]
            if c > 0 and j != e:
                if (j, e) not in relayed:
                    k = 0
                elif topo.mates(topo.chip(cores[j]), topo.chip(cores[e])):
                    k = 1 + turn[(j, e)]
                else:
                    k = 2 + turn[(j, e)]
                segs.append((k, y, c, j))
            y += c
        segs.sort()
        land, group_of, groups = {}, {}, []
        pos, cur, start = 0, [], 0
        for i, (k, y0, c, j) in enumerate(segs):
            land[j] = pos
            group_of[j] = len(groups)
            if cur and cur[-1][0] + cur[-1][2] == pos and cur[-1][1] + cur[-1][2] == y0:
                cur[-1][2] += c
            else:
                cur.append([pos, y0, c])
            pos += c
            last = i + 1 == len(segs)
            if last or (pos - start >= LEAST and (k > 0 or segs[i + 1][0] > 0)):
                groups.append({"start": start, "end": pos, "win": min(start, pos - LEAST), "stores": cur})
                cur, start = [], pos
        for k, gr in enumerate(groups):
            gr["count"] = sum(2 * eng.get((j, e), E_DIRECT) for j in group_of if group_of[j] == k)
        experts.append({"land": land, "group_of": group_of, "groups": groups})

    return {"cnt": cnt, "cores": cores, "n": n, "off": off, "tot": tot, "ncol": ncol, "flows": flows,
            "relayed": relayed, "eng": eng, "helpers": helpers, "pieces": pieces, "hulls": hulls, "experts": experts}


def _write(g, T, topo, src, dst, out_ap, in_ap, sem, k):
    rid, pid, _se = topo.addr(dst)
    g.remote_dma(out_ap, in_ap, remote_sem=sem, local_sem=T.sem.sent, pid=pid, routing_id=rid,
                 dma_engine_mask=_engines(topo.mask(src, dst), k))
    return k


def _sides(T, P, j, e, kind, q, s):
    a, b = P["off"][j][e], P["off"][j][e + 1]
    X = P["experts"][e]
    la = X["land"][j]
    lb = la + b - a
    sem = T.sem["arr%d" % X["group_of"][j]]
    if kind == 0:
        return T.lq[:, la:lb].bitcast(dt.uint8), q[:, a:b].bitcast(dt.uint8), sem
    return T.ls[:, la:lb], s[:, a:b], sem


def _deliver(g, T, topo, P, core, j, call, kind, q, s, k):
    if len(call) == 1:
        out_ap, in_ap, sem = _sides(T, P, j, call[0], kind, q, s)
        return _write(g, T, topo, core, P["cores"][call[0]], out_ap, in_ap, sem, k)
    trs = []
    for i, e in enumerate(call):
        out_ap, in_ap, sem = _sides(T, P, j, e, kind, q, s)
        rid, pid, _se = topo.addr(P["cores"][e])
        trs.append(RemoteDMATransfer(dst_ids=[DstId(rid=rid, pnc=pid)], remote_sem=sem, src=in_ap, dst=out_ap,
                                     dma_engine_mask=_engines(topo.mask(core, P["cores"][e]), k, i * k)))
    g.remote_dma_fused(trs, local_sem=T.sem.sent)
    return k * len(call)


def _helper(g, core, T, topo, P):
    for j in P["helpers"]:
        for kind in (0, 1):
            if P["helpers"][j][kind] != core:
                continue
            sent = 0
            for i, (_p, _a, _b, calls) in enumerate(P["hulls"][j]):
                g.wait_ge(T.sem["hin%d" % i], E_HOP1)
                for call in calls:
                    sent += _deliver(g, T, topo, P, core, j, call, kind, T.hq, T.hs, P["eng"][(j, call[0])])
            g.wait_ge(T.sem.sent, sent)


def rank_program(g, core, T, topo):
    P = _plan(T, topo)
    rank = T.rank_of(core)
    if rank is None:
        _helper(g, core, T, topo, P)
        return
    cnt, off = P["cnt"], P["off"]
    pieces = P["pieces"][rank]
    X = P["experts"][rank]

    for p, (a, b) in enumerate(pieces):
        g.sync.dma_start(T.xb[:, 4 * a:4 * b], T.x[:, 4 * a:4 * b]).then_inc(T.sem["ld%d" % p], 16)
    g.sync.dma_start(T.wb[:], T.w[:]).then_inc(T.sem.ldw, 16)
    for p, (a, b) in enumerate(pieces):
        g.vector.wait_ge(T.sem["ld%d" % p], 16)
        g.vector.quantize_mx(T.xq[:, a:b], T.xs[:, a:b], T.xb[:, 4 * a:4 * b]).then_inc(T.sem["q%d" % p], 1)
    g.vector.wait_ge(T.sem.ldw, 16)
    g.vector.quantize_mx(T.wq[:], T.ws[:], T.wb[:]).then_inc(T.sem.qw, 1)

    ready = []

    def need(p):
        if p not in ready:
            g.wait_ge(T.sem["q%d" % p], 1)
            ready.append(p)

    sent = 0
    for i, (p, a, b, _calls) in enumerate(P["hulls"][rank]):
        need(p)
        hc, hs = P["helpers"][rank]
        sem = T.sem["hin%d" % i]
        sent += _write(g, T, topo, core, hc, T.hq[:, a:b].bitcast(dt.uint8), T.xq[:, a:b].bitcast(dt.uint8), sem, E_HOP1)
        sent += _write(g, T, topo, core, hs, T.hs[:, a:b], T.xs[:, a:b], sem, E_HOP1)
    direct = [e for (j, e) in P["flows"] if j == rank and (j, e) not in P["relayed"]]
    direct.sort(key=lambda e: -P["tot"][e])
    for e in direct:
        for p, (a, b) in enumerate(pieces):
            if a <= off[rank][e] and off[rank][e + 1] <= b:
                need(p)
        for kind in (0, 1):
            sent += _deliver(g, T, topo, P, core, rank, [e], kind, T.xq, T.xs, E_DIRECT)
    for p in range(len(pieces)):
        need(p)

    stores = 0
    own = cnt[rank][rank]
    g.tensor.wait_ge(T.sem.qw, 1)
    if own:
        a = off[rank][rank]
        wn = max(LEAST, own)
        wa = min(a, P["ncol"] - wn)
        for p in range(len(pieces)):
            g.tensor.wait_ge(T.sem["q%d" % p], 1)
        g.tensor.matmul_mx(T.ps[:, 0:wn], T.wq[:], T.ws[:], T.xq[:, wa:wa + wn], T.xs[:, wa:wa + wn],
                           True, True).then_inc(T.sem.mmo, 1)
        g.vector.wait_ge(T.sem.mmo, 1)
        g.vector.tensor_copy(T.so[:, 0:own], T.ps[:, a - wa:a - wa + own]).then_inc(T.sem.cpo, 1)
        y0 = sum(cnt[j][rank] for j in range(rank))
        g.sync.wait_ge(T.sem.cpo, 1)
        g.sync.dma_start(T.y[:, y0:y0 + own], T.so[:, 0:own]).then_inc(T.sem.st, 16)
        stores += 1
    for k, gr in enumerate(X["groups"]):
        base = (k + 1) * BANK
        wa, s0, s1 = gr["win"], gr["start"], gr["end"]
        g.tensor.wait_ge(T.sem["arr%d" % k], gr["count"])
        g.tensor.matmul_mx(T.ps[:, base:base + s1 - wa], T.wq[:], T.ws[:], T.lq[:, wa:s1], T.ls[:, wa:s1],
                           True, True).then_inc(T.sem["mm%d" % k], 1)
        src = T.ps[:, base + s0 - wa:base + s1 - wa]
        if k % 2 == 0:
            g.vector.wait_ge(T.sem["mm%d" % k], 1)
            g.vector.tensor_copy(T.sg[:, s0:s1], src).then_inc(T.sem["cp%d" % k], 1)
        else:
            g.scalar.wait_ge(T.sem["mm%d" % k], 1)
            g.scalar.activation(T.sg[:, s0:s1], src, ActivationFunctionType.Copy).then_inc(T.sem["cp%d" % k], 1)
        queues = [g.sync, g.scalar] if k % 2 == 0 else [g.scalar, g.sync]
        used = []
        for i, (la, y0, c) in enumerate(gr["stores"]):
            qu = queues[i % 2]
            if i % 2 not in used:
                qu.wait_ge(T.sem["cp%d" % k], 1)
                used.append(i % 2)
            qu.dma_start(T.y[:, y0:y0 + c], T.sg[:, la:la + c]).then_inc(T.sem.st, 16)
            stores += 1

    g.wait_ge(T.sem.sent, sent)
    g.wait_ge(T.sem.st, 16 * stores)
